import numpy as np
import ml_dtypes


def mxq(x, axis, fmt="e4m3"):
    dtype, down = {"e4m3": (ml_dtypes.float8_e4m3fn, 7), "e5m2": (ml_dtypes.float8_e5m2, 14)}[fmt]
    v = np.moveaxis(np.asarray(x, np.float32).astype(ml_dtypes.bfloat16).astype(np.float64), axis, -1)
    blocks = v.reshape(v.shape[:-1] + (-1, 32))
    amax = np.abs(blocks).max(-1, keepdims=True)
    byte = np.maximum(np.where(amax > 0, np.frexp(amax)[1] - 1 + 127, 0) - down, 1)
    scale = np.exp2(byte - 127.0)
    codes = (blocks / scale).astype(np.float32).astype(dtype).astype(np.float64)
    return np.moveaxis((codes * scale).reshape(v.shape), -1, axis)


WIDE = False


def mx_kscale(k):
    if not WIDE:
        return np.ones(k)
    levels = np.array([10, -10, 5, -5, 0])
    if k % 512:
        return np.exp2(np.random.permutation(np.resize(levels, k // 32))).repeat(32)
    a = np.empty((k // 512, 16))
    for p in range(k // 512):
        a[p, :8] = np.random.permutation(np.resize(levels, 8))
        for g in range(8):
            far = levels[np.abs(levels - a[p, g]) >= 10]
            a[p, g + 8] = far[np.random.randint(len(far))]
    return np.exp2(a.ravel()).repeat(32)


def f64(x):
    return np.asarray(x).astype(np.float64)


def striped(idx):
    return np.tile(idx.reshape(-1, 16).T, (8, 1)).astype(np.uint16)


def unstriped(offs):
    return offs[:16].T.reshape(-1).astype(np.int64)


def pack_weight(w):
    k, n = w.shape
    w = f64(np.asarray(w, np.float32).astype(ml_dtypes.bfloat16)).reshape(k // 32, 32, n)
    amax = np.abs(w).max(1)
    byte = np.clip(np.where(amax > 0, np.frexp(amax)[1] - 1 + 127 - 7, 1), 1, 254)
    scaled = (w * np.exp2(127.0 - byte)[:, None, :]).reshape(k, n).astype(np.float32)
    words = np.ascontiguousarray(scaled.reshape(k // 512, 128, 4, n).transpose(0, 1, 3, 2)).astype(ml_dtypes.float8_e4m3fn).view(np.uint8)
    return words, np.ascontiguousarray(byte.astype(np.uint8).reshape(k // 512, 16, n))


def unpack_weight(words, scales):
    g, p, n, _ = words.shape
    vals = np.ascontiguousarray(words).view(ml_dtypes.float8_e4m3fn).astype(np.float64) * np.repeat(np.exp2(scales.astype(np.float64) - 127.0), 8, axis=1)[..., None]
    return vals.transpose(0, 1, 3, 2).reshape(g * 512, n)


def relu(v):
    return np.maximum(v, 0.0)


K, T, S, V, D, N, H = 1024, 4096, 1024, 512, 8, 128, 512
P = 2 ** 7


def setup_inputs():
    n = np.random.standard_normal
    s = mx_kscale(K)[:, None]
    u = mx_kscale(H)
    packed_xT = pack_weight(n((K, T)) * s)
    return {
        "x_words": packed_xT[0],
        "x_scales": packed_xT[1],
        "hT": (n((K, V)) / np.sqrt(K) / s).astype(np.float32),
        "qn": (np.tile(np.random.uniform(0.5, 1.5, T), (P, 1))).astype(np.float32),
        "own": (np.random.uniform(0.5, 1.5, (V, 1))).astype(np.float32),
        "idf": (np.random.uniform(0.5, 1.5, (H, 1)) * u[:, None]).astype(np.float32),
        "bag": (np.random.uniform(0.0, 1.0, (H, N)) ** 6 / 40 / u[:, None]).astype(np.float32),
        "offs": striped(np.random.permutation(T)[:S]),
    }


def reference(x_words, x_scales, hT, qn, own, idf, bag, offs):
    hTq = mxq(f64(hT), 0, "e4m3")
    xq = unpack_weight(x_words, x_scales)[:, unstriped(offs)]
    dd = np.sqrt(relu(f64(qn)[:1][:, unstriped(offs)] - (1.5 * (hTq.T @ xq)) + f64(own)) + 0.01)
    near = dd.reshape(len(dd), -1, D).min(axis=2)
    z = f64(idf) * near
    return np.exp(-1.0 * ((mxq(f64(bag), 0, "e4m3").T @ mxq(z, 0, "e4m3"))))

@@ -1,0 +1,216 @@
+from contextlib import ExitStack
+
+import concourse.mybir as mybir
+from concourse.masks import make_identity
+
+K, T, S, V, D, N = 1024, 4096, 1024, 512, 8, 128
+FLOPS = 2 * K * V * S + 2 * V * N * (S // D)
+BYTES = K * T + (K // 32) * T + 4 * (K * V + T + 2 * V + V * N + N * (S // D)) + 2 * 128 * (S // 16)
+
+F32 = mybir.dt.float32
+BF16 = mybir.dt.bfloat16
+I32 = mybir.dt.int32
+U32 = mybir.dt.uint32
+U16 = mybir.dt.uint16
+U8 = mybir.dt.uint8
+FP8X4 = mybir.dt.float8_e4m3fn_x4
+ALU = mybir.AluOpType
+ACT = mybir.ActivationFunctionType
+AX = mybir.AxisListType
+
+P = 128
+PACK = 4
+PASSES = 2
+HALVES = 2
+GH = 64
+PAIRS = 4
+TC = 256
+CHUNKS = 2
+
+
+def tile_picked_yrwmd_sim_p_kernel(tc, x_words, x_scales, hT, qn, own, idf, bag, offs, out):
+    nc = tc.nc
+    with ExitStack() as ctx:
+        held = ctx.enter_context(tc.tile_pool(name="held", bufs=1))
+        keep = ctx.enter_context(tc.tile_pool(name="keep", bufs=1))
+        psum = ctx.enter_context(tc.psum_pool(name="psum", bufs=8))
+
+        offsets = held.tile([P, S // 16], U16, name="offsets")
+        nc.sync.dma_start(offsets[:], offs)
+
+        def load_words(o, tag):
+            w = keep.tile([P, T], U32, name="xw%d" % o, tag=tag, align_bytes=64)
+            nc.sync.dma_start(w[:].bitcast(I32), x_words[o].rearrange("p c r -> p (c r)").bitcast(I32))
+            return w
+
+        def h_rows(o, c):
+            return hT[512 * o:512 * (o + 1), TC * c:TC * (c + 1)].rearrange("(p j) t -> p j t", j=PACK)
+
+        sw = keep.tile([P, T], U8, name="sw", tag="w1", align_bytes=64)
+        nc.sync.dma_start(sw[0:32, :].bitcast(I32), x_scales.rearrange("o q c -> (o q) c").bitcast(I32))
+        xw0 = load_words(0, "w0")
+        h00 = keep.tile([P, PACK * TC], F32, name="h00")
+        nc.sync.dma_start(h00[:].rearrange("p (j t) -> p j t", j=PACK), h_rows(0, 0))
+
+        nc.vector.memset(sw[32:64, :].bitcast(I32), 0)
+        nc.vector.memset(sw[64:128, :].bitcast(I32), 0)
+        qw = keep.tile([P, T], F32, name="qw", tag="wq", align_bytes=64)
+        nc.vector.memset(qw[:].bitcast(I32), 0)
+        nc.scalar.dma_start(qw[0:1, :], qn[0:1, :])
+
+        ident = keep.tile([P, P], F32, name="ident")
+        make_identity(nc, ident[:])
+        sp = [keep.tile([P, S], U8, name="sp%d" % o, align_bytes=64) for o in range(PASSES)]
+        for o in range(PASSES):
+            nc.gpsimd.memset(sp[o][:].bitcast(I32), 0)
+        warm = keep.tile([P, 1], F32, name="warm")
+        nc.scalar.activation(warm[:], ident[:, 0:1], ACT.Sqrt, bias=1.0)
+
+        sg = keep.tile([P, S], U8, name="sg", align_bytes=64)
+        nc.vector.tensor_copy(sg[:], sw[:].indirect(offsets[:]))
+        xw1 = load_words(1, "w1")
+        sd = keep.tile([P, S], U8, name="sd", align_bytes=64)
+        nc.vector.tensor_copy(
+            sd[:].rearrange("p (h f g e) -> p h f g e", h=HALVES, f=PAIRS, e=2),
+            sg[:].rearrange("p (h g f e) -> p h f g e", h=HALVES, f=PAIRS, e=2))
+        for o in range(PASSES):
+            queue = nc.scalar if o == 0 else nc.gpsimd
+            for q in range(4):
+                queue.dma_start(sp[o][32 * q:32 * q + 4, :].bitcast(I32),
+                                sd[16 * o + 4 * q:16 * o + 4 * q + 4, :].bitcast(I32))
+
+        xg = {}
+
+        def gather_words(o, w):
+            for h in range(HALVES):
+                t = keep.tile([P, 512], U32, name="xg%d%d" % (o, h), tag=("wq" if (o, h) == (1, 0) else "xg%d%d" % (o, h)), align_bytes=64)
+                nc.vector.tensor_copy(
+                    t[:].rearrange("p (f g e) -> p g f e", f=PAIRS, e=2),
+                    w[:].indirect(offsets[:, 32 * h:32 * (h + 1)]))
+                xg[(o, h)] = t
+
+        gather_words(0, xw0)
+        qg = keep.tile([P, S], F32, name="qg", align_bytes=64)
+        nc.vector.tensor_copy(qg[:], qw[:].indirect(offsets[:]))
+
+        late = keep.tile([P, T], F32, name="late", tag="w0", align_bytes=64)
+        raw = {(0, 0): h00[:]}
+        for n, (o, c) in enumerate([(1, 0), (0, 1), (1, 1)]):
+            raw[(o, c)] = late[:, 1024 * n:1024 * (n + 1)]
+            nc.sync.dma_start(raw[(o, c)].rearrange("p (j t) -> p j t", j=PACK), h_rows(o, c))
+        bag_raw = late[:, 3072:3584]
+        nc.sync.dma_start(bag_raw, bag.rearrange("(p j) m -> p (j m)", j=PACK))
+        own_t = late[:, 3584:3588]
+        idf_t = late[:, 3600:3604]
+        nc.sync.dma_start(own_t, own.rearrange("(p i) o -> p (i o)", i=PACK))
+        nc.sync.dma_start(idf_t, idf.rearrange("(p i) o -> p (i o)", i=PACK))
+
+        qp = keep.tile([P, S], F32, name="qp", align_bytes=64)
+        for h in range(HALVES):
+            nc.scalar.activation(
+                qp[:, 512 * h:512 * (h + 1)].rearrange("p (f g e) -> p f g e", f=PAIRS, e=2),
+                qg[:, 512 * h:512 * (h + 1)].rearrange("p (g f e) -> p f g e", f=PAIRS, e=2),
+                ACT.Copy, scale=-1.0 / 1.5)
+        nq = keep.tile([P, HALVES * PAIRS], F32, name="nq")
+        for h in range(HALVES):
+            qt = psum.tile([P, PAIRS, P], F32, name="qt", tag="bank")
+            for f in range(PAIRS):
+                nc.tensor.transpose(qt[:, f, :], qp[:, 512 * h + P * f:512 * h + P * (f + 1)], ident[:])
+            nc.scalar.copy(nq[:, PAIRS * h:PAIRS * (h + 1)], qt[:, :, 0])
+
+        def round_and_group(name, src, width):
+            grouped = keep.tile([P, PACK * width], BF16, name=name + "_b", align_bytes=64)
+            nc.scalar.copy(
+                grouped[:].rearrange("p (c i j) -> p c j i", i=4, j=PACK),
+                src.rearrange("p (j c i) -> p c j i", i=4, j=PACK))
+            return grouped
+
+        def quantize(name, grouped, width):
+            codes = keep.tile([P, width], U32, name=name + "_c", align_bytes=64)
+            scales = keep.tile([P, width], U8, name=name + "_s", align_bytes=64)
+            nc.vector.quantize_mx(out=codes[:].bitcast(FP8X4), scales=scales[:], in_=grouped[:])
+            return codes, scales
+
+        hq = {}
+
+        def make_h(o, c):
+            name = "h%d%d" % (o, c)
+            hq[(o, c)] = quantize(name, round_and_group(name, raw[(o, c)], TC), TC)
+
+        banks = {}
+
+        def product(o, c, h):
+            codes, scales = hq[(o, c)]
+            for f in range(PAIRS):
+                if o == 0:
+                    banks[(c, h, f)] = psum.tile([P, TC], F32, name="s", tag="bank")
+                col = 512 * h + P * f
+                nc.tensor.matmul_mx(
+                    out=banks[(c, h, f)][:],
+                    lhsT=xg[(o, h)][:, P * f:P * (f + 1)].bitcast(FP8X4),
+                    lhsT_scale=sp[o][:, col:col + P],
+                    rhs=codes[:].bitcast(FP8X4), rhs_scale=scales[:],
+                    start=(o == 0), stop=(o == PASSES - 1))
+
+        best = [keep.tile([P, PACK, P], F32, name="best%d" % h) for h in range(HALVES)]
+
+        def nearest(c):
+            run = {}
+            for f in range(PAIRS):
+                for h in range(HALVES):
+                    sums = banks[(c, h, f)][:].rearrange("p (m i) -> p i m", i=PACK)
+                    bias = nq[:, PAIRS * h + f:PAIRS * h + f + 1]
+                    if f == PAIRS - 1:
+                        dst = best[h][:, :, 64 * c:64 * (c + 1)]
+                    else:
+                        part = keep.tile([P, PACK, 64], F32, name="part%d%d%d" % (c, h, f))
+                        dst = part[:]
+                    if f == 0:
+                        nc.scalar.activation(dst, sums, ACT.Identity, bias=bias)
+                    else:
+                        nc.vector.scalar_tensor_tensor(dst, sums, bias, run[h], ALU.add, ALU.max)
+                    run[h] = dst
+
+        make_h(0, 0)
+        for h in range(HALVES):
+            product(0, 0, h)
+        gather_words(1, xw1)
+        make_h(1, 0)
+        for h in range(HALVES):
+            product(1, 0, h)
+        make_h(0, 1)
+        nearest(0)
+        make_h(1, 1)
+        for h in range(HALVES):
+            product(0, 1, h)
+        for h in range(HALVES):
+            product(1, 1, h)
+        bag_c, bag_s = quantize("bag", round_and_group("bag", bag_raw, N), N)
+        nearest(1)
+
+        z = keep.tile([P, N * PACK], BF16, name="z", align_bytes=64)
+        roots = []
+        for h in range(HALVES):
+            turned = psum.tile([P, PACK, P], F32, name="turned", tag="bank")
+            for i in range(PACK):
+                nc.tensor.transpose(turned[:, i, :], best[h][:, i, :], ident[:])
+            near = keep.tile([P, PACK, GH], F32, name="near%d" % h)
+            nc.vector.tensor_reduce(near[:], turned[:].rearrange("p i (g e) -> p i g e", e=2), AX.X, ALU.max)
+            dist = keep.tile([P, PACK, GH], F32, name="dist%d" % h)
+            for i in range(PACK):
+                nc.scalar.activation(dist[:, i, :], near[:, i, :], ACT.Relu, bias=own_t[:, i:i + 1], scale=-1.5)
+            root = keep.tile([P, PACK, GH], F32, name="root%d" % h)
+            nc.scalar.activation(root[:], dist[:], ACT.Sqrt, bias=0.01)
+            roots.append(root)
+        for h in range(HALVES):
+            nc.vector.tensor_tensor(
+                z[:, PACK * GH * h:PACK * GH * (h + 1)].rearrange("p (g i) -> p g i", i=PACK),
+                roots[h][:].rearrange("p i g -> p g i"),
+                idf_t.unsqueeze(1).to_broadcast([P, GH, PACK]), ALU.mult)
+        z_c, z_s = quantize("z", z, N)
+        cost = psum.tile([P, N], F32, name="cost", tag="bank")
+        nc.tensor.matmul_mx(out=cost[:], lhsT=bag_c[:].bitcast(FP8X4), lhsT_scale=bag_s[:],
+                            rhs=z_c[:].bitcast(FP8X4), rhs_scale=z_s[:], start=True, stop=True)
+        result = keep.tile([P, N], F32, name="result")
+        nc.scalar.activation(result[:], cost[:], ACT.Exp, scale=-1.0)
+        nc.sync.dma_start(out, result[:])

@@ -46,55 +46,85 @@ def tile_picked_yrwmd_sim_p_kernel(tc, x_words, x_scales, hT, qn, own, idf, bag,
         def h_rows(o, c):
             return hT[512 * o:512 * (o + 1), TC * c:TC * (c + 1)].rearrange("(p j) t -> p j t", j=PACK)
 
-        sw = keep.tile([P, T], U8, name="sw", tag="w1", align_bytes=64)
+        sw = keep.tile([P, T], U8, name="sw", align_bytes=64)
         nc.sync.dma_start(sw[0:32, :].bitcast(I32), x_scales.rearrange("o q c -> (o q) c").bitcast(I32))
         xw0 = load_words(0, "w0")
-        h00 = keep.tile([P, PACK * TC], F32, name="h00")
+        h00 = keep.tile([P, PACK * TC], F32, name="h00", tag="h00", align_bytes=64)
         nc.sync.dma_start(h00[:].rearrange("p (j t) -> p j t", j=PACK), h_rows(0, 0))
 
+        qw = keep.tile([P, T], F32, name="qw", tag="wq", align_bytes=64)
+        zero = keep.tile([P, 1], F32, name="zero", tag="w1", align_bytes=64)
+        nc.vector.memset(zero[:], 0.0)
+        warm = keep.tile([P, 1], F32, name="warm")
+        nc.scalar.activation(warm[:], zero[:], ACT.Sqrt, bias=1.0)
+        nc.scalar.copy(qw[:, 0:2048], zero[:].to_broadcast([P, 2048]))
         nc.vector.memset(sw[32:64, :].bitcast(I32), 0)
         nc.vector.memset(sw[64:128, :].bitcast(I32), 0)
-        qw = keep.tile([P, T], F32, name="qw", tag="wq", align_bytes=64)
-        nc.vector.memset(qw[:].bitcast(I32), 0)
-        nc.scalar.dma_start(qw[0:1, :], qn[0:1, :])
+        nc.vector.memset(qw[:, 2048:3072], 0.0)
+        nc.gpsimd.memset(qw[:, 3072:4096], 0.0)
+        nc.sync.dma_start(qw[0:1, :], qn[0:1, :])
+        xw1 = load_words(1, "w1")
 
+        sp = [keep.tile([P, S], U8, name="sp0", align_bytes=64)]
+        nc.gpsimd.memset(sp[0][:].bitcast(I32), 0)
         ident = keep.tile([P, P], F32, name="ident")
         make_identity(nc, ident[:])
-        sp = [keep.tile([P, S], U8, name="sp%d" % o, align_bytes=64) for o in range(PASSES)]
-        for o in range(PASSES):
-            nc.gpsimd.memset(sp[o][:].bitcast(I32), 0)
-        warm = keep.tile([P, 1], F32, name="warm")
-        nc.scalar.activation(warm[:], ident[:, 0:1], ACT.Sqrt, bias=1.0)
 
         sg = keep.tile([P, S], U8, name="sg", align_bytes=64)
         nc.vector.tensor_copy(sg[:], sw[:].indirect(offsets[:]))
-        xw1 = load_words(1, "w1")
         sd = keep.tile([P, S], U8, name="sd", align_bytes=64)
         nc.vector.tensor_copy(
             sd[:].rearrange("p (h f g e) -> p h f g e", h=HALVES, f=PAIRS, e=2),
             sg[:].rearrange("p (h g f e) -> p h f g e", h=HALVES, f=PAIRS, e=2))
-        for o in range(PASSES):
-            queue = nc.scalar if o == 0 else nc.gpsimd
-            for q in range(4):
-                queue.dma_start(sp[o][32 * q:32 * q + 4, :].bitcast(I32),
-                                sd[16 * o + 4 * q:16 * o + 4 * q + 4, :].bitcast(I32))
 
+        def place_scales(o):
+            for q in range(4):
+                nc.scalar.dma_start(sp[o][32 * q:32 * q + 4, :].bitcast(I32),
+                                    sd[16 * o + 4 * q:16 * o + 4 * q + 4, :].bitcast(I32))
+
+        place_scales(0)
         xg = {}
 
-        def gather_words(o, w):
-            for h in range(HALVES):
-                t = keep.tile([P, 512], U32, name="xg%d%d" % (o, h), tag=("wq" if (o, h) == (1, 0) else "xg%d%d" % (o, h)), align_bytes=64)
-                nc.vector.tensor_copy(
-                    t[:].rearrange("p (f g e) -> p g f e", f=PAIRS, e=2),
-                    w[:].indirect(offsets[:, 32 * h:32 * (h + 1)]))
-                xg[(o, h)] = t
+        def gather_words(o, h, w, tag):
+            t = keep.tile([P, 512], U32, name="xg%d%d" % (o, h), tag=tag, align_bytes=64)
+            nc.vector.tensor_copy(
+                t[:].rearrange("p (f g e) -> p g f e", f=PAIRS, e=2),
+                w[:].indirect(offsets[:, 32 * h:32 * (h + 1)]))
+            xg[(o, h)] = t
 
-        gather_words(0, xw0)
-        qg = keep.tile([P, S], F32, name="qg", align_bytes=64)
-        nc.vector.tensor_copy(qg[:], qw[:].indirect(offsets[:]))
+        def round_and_group(name, src, width, tag):
+            grouped = keep.tile([P, PACK * width], BF16, name=name + "_b", tag=tag, align_bytes=64)
+            nc.scalar.copy(
+                grouped[:].rearrange("p (c i j) -> p c j i", i=4, j=PACK),
+                src.rearrange("p (j c i) -> p c j i", i=4, j=PACK))
+            return grouped
 
-        late = keep.tile([P, T], F32, name="late", tag="w0", align_bytes=64)
+        def quantize(name, grouped, width, tag):
+            codes = keep.tile([P, width], U32, name=name + "_c", tag=tag, align_bytes=64)
+            scales = keep.tile([P, width], U8, name=name + "_s", align_bytes=64)
+            nc.vector.quantize_mx(out=codes[:].bitcast(FP8X4), scales=scales[:], in_=grouped[:])
+            return codes, scales
+
+        hq = {}
+
+        hb = {}
+
+        def round_h(o, c):
+            name = "h%d%d" % (o, c)
+            hb[(o, c)] = round_and_group(name, raw[(o, c)], TC, name + "_b")
+
+        def quantize_h(o, c, tag):
+            hq[(o, c)] = quantize("h%d%d" % (o, c), hb[(o, c)], TC, tag)
+
         raw = {(0, 0): h00[:]}
+        gather_words(0, 0, xw0, "xg00")
+        qg = keep.tile([P, S], F32, name="qg", tag="qg", align_bytes=64)
+        nc.vector.tensor_copy(qg[:], qw[:].indirect(offsets[:]))
+        gather_words(0, 1, xw0, "wq")
+        round_h(0, 0)
+        quantize_h(0, 0, "h00_c")
+
+        late = keep.tile([P, T + S], F32, name="late", tag="h00", align_bytes=64)
         for n, (o, c) in enumerate([(1, 0), (0, 1), (1, 1)]):
             raw[(o, c)] = late[:, 1024 * n:1024 * (n + 1)]
             nc.sync.dma_start(raw[(o, c)].rearrange("p (j t) -> p j t", j=PACK), h_rows(o, c))
@@ -105,12 +135,15 @@ def tile_picked_yrwmd_sim_p_kernel(tc, x_words, x_scales, hT, qn, own, idf, bag,
         nc.sync.dma_start(own_t, own.rearrange("(p i) o -> p (i o)", i=PACK))
         nc.sync.dma_start(idf_t, idf.rearrange("(p i) o -> p (i o)", i=PACK))
 
-        qp = keep.tile([P, S], F32, name="qp", align_bytes=64)
+        qp = late[:, T:T + S]
         for h in range(HALVES):
             nc.scalar.activation(
                 qp[:, 512 * h:512 * (h + 1)].rearrange("p (f g e) -> p f g e", f=PAIRS, e=2),
                 qg[:, 512 * h:512 * (h + 1)].rearrange("p (g f e) -> p f g e", f=PAIRS, e=2),
                 ACT.Copy, scale=-1.0 / 1.5)
+        sp.append(keep.tile([P, S], U8, name="sp1", tag="qg", align_bytes=64))
+        nc.vector.memset(sp[1][:].bitcast(I32), 0)
+        place_scales(1)
         nq = keep.tile([P, HALVES * PAIRS], F32, name="nq")
         for h in range(HALVES):
             qt = psum.tile([P, PAIRS, P], F32, name="qt", tag="bank")
@@ -118,75 +151,62 @@ def tile_picked_yrwmd_sim_p_kernel(tc, x_words, x_scales, hT, qn, own, idf, bag,
                 nc.tensor.transpose(qt[:, f, :], qp[:, 512 * h + P * f:512 * h + P * (f + 1)], ident[:])
             nc.scalar.copy(nq[:, PAIRS * h:PAIRS * (h + 1)], qt[:, :, 0])
 
-        def round_and_group(name, src, width):
-            grouped = keep.tile([P, PACK * width], BF16, name=name + "_b", align_bytes=64)
-            nc.scalar.copy(
-                grouped[:].rearrange("p (c i j) -> p c j i", i=4, j=PACK),
-                src.rearrange("p (j c i) -> p c j i", i=4, j=PACK))
-            return grouped
-
-        def quantize(name, grouped, width):
-            codes = keep.tile([P, width], U32, name=name + "_c", align_bytes=64)
-            scales = keep.tile([P, width], U8, name=name + "_s", align_bytes=64)
-            nc.vector.quantize_mx(out=codes[:].bitcast(FP8X4), scales=scales[:], in_=grouped[:])
-            return codes, scales
-
-        hq = {}
-
-        def make_h(o, c):
-            name = "h%d%d" % (o, c)
-            hq[(o, c)] = quantize(name, round_and_group(name, raw[(o, c)], TC), TC)
-
         banks = {}
 
-        def product(o, c, h):
+        def product(o, c):
             codes, scales = hq[(o, c)]
             for f in range(PAIRS):
-                if o == 0:
-                    banks[(c, h, f)] = psum.tile([P, TC], F32, name="s", tag="bank")
-                col = 512 * h + P * f
-                nc.tensor.matmul_mx(
-                    out=banks[(c, h, f)][:],
-                    lhsT=xg[(o, h)][:, P * f:P * (f + 1)].bitcast(FP8X4),
-                    lhsT_scale=sp[o][:, col:col + P],
-                    rhs=codes[:].bitcast(FP8X4), rhs_scale=scales[:],
-                    start=(o == 0), stop=(o == PASSES - 1))
+                for h in range(HALVES):
+                    if o == 0:
+                        banks[(c, h, f)] = psum.tile([P, TC], F32, name="s", tag="bank")
+                    col = 512 * h + P * f
+                    nc.tensor.matmul_mx(
+                        out=banks[(c, h, f)][:],
+                        lhsT=xg[(o, h)][:, P * f:P * (f + 1)].bitcast(FP8X4),
+                        lhsT_scale=sp[o][:, col:col + P],
+                        rhs=codes[:].bitcast(FP8X4), rhs_scale=scales[:],
+                        start=(o == 0), stop=(o == PASSES - 1))
 
         best = [keep.tile([P, PACK, P], F32, name="best%d" % h) for h in range(HALVES)]
 
-        def nearest(c):
-            run = {}
-            for f in range(PAIRS):
-                for h in range(HALVES):
-                    sums = banks[(c, h, f)][:].rearrange("p (m i) -> p i m", i=PACK)
-                    bias = nq[:, PAIRS * h + f:PAIRS * h + f + 1]
-                    if f == PAIRS - 1:
-                        dst = best[h][:, :, 64 * c:64 * (c + 1)]
-                    else:
-                        part = keep.tile([P, PACK, 64], F32, name="part%d%d%d" % (c, h, f))
-                        dst = part[:]
-                    if f == 0:
-                        nc.scalar.activation(dst, sums, ACT.Identity, bias=bias)
-                    else:
-                        nc.vector.scalar_tensor_tensor(dst, sums, bias, run[h], ALU.add, ALU.max)
-                    run[h] = dst
+        run = {}
 
-        make_h(0, 0)
+        def nearest(c, f):
+            for h in range(HALVES):
+                sums = banks[(c, h, f)][:].rearrange("p (m i) -> p i m", i=PACK)
+                bias = nq[:, PAIRS * h + f:PAIRS * h + f + 1]
+                if f == PAIRS - 1:
+                    dst = best[h][:, :, 64 * c:64 * (c + 1)]
+                else:
+                    part = keep.tile([P, PACK, 64], F32, name="part%d%d%d" % (c, h, f), align_bytes=64)
+                    dst = part[:]
+                if f > 0:
+                    nc.vector.scalar_tensor_tensor(dst, sums, bias, run[h], ALU.add, ALU.max)
+                elif c == 0:
+                    nc.vector.tensor_scalar(dst, sums, bias, None, ALU.add)
+                else:
+                    nc.scalar.activation(dst, sums, ACT.Identity, bias=bias)
+                run[h] = dst
+
+        product(0, 0)
         for h in range(HALVES):
-            product(0, 0, h)
-        gather_words(1, xw1)
-        make_h(1, 0)
-        for h in range(HALVES):
-            product(1, 0, h)
-        make_h(0, 1)
-        nearest(0)
-        make_h(1, 1)
-        for h in range(HALVES):
-            product(0, 1, h)
-        for h in range(HALVES):
-            product(1, 1, h)
-        bag_c, bag_s = quantize("bag", round_and_group("bag", bag_raw, N), N)
-        nearest(1)
+            gather_words(1, h, xw1, "xg1%d" % h)
+        round_h(1, 0)
+        quantize_h(1, 0, "h10_c")
+        product(1, 0)
+        round_h(0, 1)
+        round_h(1, 1)
+        nearest(0, 0)
+        nearest(0, 1)
+        quantize_h(0, 1, "part000")
+        nearest(0, 2)
+        quantize_h(1, 1, "part001")
+        nearest(0, 3)
+        product(0, 1)
+        product(1, 1)
+        for f in range(PAIRS):
+            nearest(1, f)
+        bag_c, bag_s = quantize("bag", round_and_group("bag", bag_raw, N, "part110"), N, "bag_c")
 
         z = keep.tile([P, N * PACK], BF16, name="z", align_bytes=64)
         roots = []
@@ -207,7 +227,7 @@ def tile_picked_yrwmd_sim_p_kernel(tc, x_words, x_scales, hT, qn, own, idf, bag,
                 z[:, PACK * GH * h:PACK * GH * (h + 1)].rearrange("p (g i) -> p g i", i=PACK),
                 roots[h][:].rearrange("p i g -> p g i"),
                 idf_t.unsqueeze(1).to_broadcast([P, GH, PACK]), ALU.mult)
-        z_c, z_s = quantize("z", z, N)
+        z_c, z_s = quantize("z", z, N, "z_c")
         cost = psum.tile([P, N], F32, name="cost", tag="bank")
         nc.tensor.matmul_mx(out=cost[:], lhsT=bag_c[:].bitcast(FP8X4), lhsT_scale=bag_s[:],
                             rhs=z_c[:].bitcast(FP8X4), rhs_scale=z_s[:], start=True, stop=True)

@@ -23,6 +23,7 @@ PACK = 4
 PASSES = 2
 HALVES = 2
 GH = 64
+G = 128
 PAIRS = 4
 TC = 256
 CHUNKS = 2
@@ -33,6 +34,8 @@ def tile_picked_yrwmd_sim_p_kernel(tc, x_words, x_scales, hT, qn, own, idf, bag,
     with ExitStack() as ctx:
         held = ctx.enter_context(tc.tile_pool(name="held", bufs=1))
         keep = ctx.enter_context(tc.tile_pool(name="keep", bufs=1))
+        reuse = ctx.enter_context(tc.tile_pool(name="reuse", bufs=1))
+        reuse2 = ctx.enter_context(tc.tile_pool(name="reuse2", bufs=1))
         psum = ctx.enter_context(tc.psum_pool(name="psum", bufs=8))
 
         offsets = held.tile([P, S // 16], U16, name="offsets")
@@ -52,7 +55,7 @@ def tile_picked_yrwmd_sim_p_kernel(tc, x_words, x_scales, hT, qn, own, idf, bag,
         h00 = keep.tile([P, PACK * TC], F32, name="h00", tag="h00", align_bytes=64)
         nc.sync.dma_start(h00[:].rearrange("p (j t) -> p j t", j=PACK), h_rows(0, 0))
 
-        qw = keep.tile([P, T], F32, name="qw", tag="wq", align_bytes=64)
+        qw = reuse.tile([P, T], F32, name="qw", offset=0, align_bytes=64)
         zero = keep.tile([P, 1], F32, name="zero", tag="w1", align_bytes=64)
         nc.vector.memset(zero[:], 0.0)
         warm = keep.tile([P, 1], F32, name="warm")
@@ -65,35 +68,36 @@ def tile_picked_yrwmd_sim_p_kernel(tc, x_words, x_scales, hT, qn, own, idf, bag,
         nc.sync.dma_start(qw[0:1, :], qn[0:1, :])
         xw1 = load_words(1, "w1")
 
-        sp = [keep.tile([P, S], U8, name="sp0", align_bytes=64)]
-        nc.gpsimd.memset(sp[0][:].bitcast(I32), 0)
+        sp1 = keep.tile([P, S], U8, name="sp1", align_bytes=64)
+        nc.gpsimd.memset(sp1[:].bitcast(I32), 0)
         ident = keep.tile([P, P], F32, name="ident")
         make_identity(nc, ident[:])
 
         sg = keep.tile([P, S], U8, name="sg", align_bytes=64)
         nc.vector.tensor_copy(sg[:], sw[:].indirect(offsets[:]))
         sd = keep.tile([P, S], U8, name="sd", align_bytes=64)
-        nc.vector.tensor_copy(
-            sd[:].rearrange("p (h f g e) -> p h f g e", h=HALVES, f=PAIRS, e=2),
-            sg[:].rearrange("p (h g f e) -> p h f g e", h=HALVES, f=PAIRS, e=2))
+        nc.vector.tensor_copy(sd[:].rearrange("p (d g) -> p d g", d=D), sg[:].rearrange("p (g d) -> p d g", d=D))
+        sp = [sd, sp1]
+        moves = [(o, q) for o in range(PASSES) for q in range(4) if (o, q) != (0, 0)]
+        for n, (o, q) in enumerate(moves):
+            queue = nc.scalar if n < 4 else nc.gpsimd
+            queue.dma_start(sp[o][32 * q:32 * q + 4, :].bitcast(I32),
+                            sd[16 * o + 4 * q:16 * o + 4 * q + 4, :].bitcast(I32))
 
-        def place_scales(o):
-            for q in range(4):
-                nc.scalar.dma_start(sp[o][32 * q:32 * q + 4, :].bitcast(I32),
-                                    sd[16 * o + 4 * q:16 * o + 4 * q + 4, :].bitcast(I32))
+        xd = {}
 
-        place_scales(0)
-        xg = {}
+        def gather_words(o, w):
+            t = keep.tile([P, S], U32, name="xg%d" % o, align_bytes=64)
+            nc.vector.tensor_copy(t[:], w[:].indirect(offsets[:]))
+            return t
 
-        def gather_words(o, h, w, tag):
-            t = keep.tile([P, 512], U32, name="xg%d%d" % (o, h), tag=tag, align_bytes=64)
+        def deal_words(o, picked, u, t):
             nc.vector.tensor_copy(
-                t[:].rearrange("p (f g e) -> p g f e", f=PAIRS, e=2),
-                w[:].indirect(offsets[:, 32 * h:32 * (h + 1)]))
-            xg[(o, h)] = t
+                t[:].bitcast(I32).rearrange("p d (b g) -> p b d g", g=4),
+                picked[:].bitcast(I32).rearrange("p (b g d) -> p b d g", g=4, d=D)[:, :, 4 * u:4 * (u + 1), :])
+            xd[(o, u)] = t
 
-        def round_and_group(name, src, width, tag):
-            grouped = keep.tile([P, PACK * width], BF16, name=name + "_b", tag=tag, align_bytes=64)
+        def round_and_group(grouped, src):
             nc.scalar.copy(
                 grouped[:].rearrange("p (c i j) -> p c j i", i=4, j=PACK),
                 src.rearrange("p (j c i) -> p c j i", i=4, j=PACK))
@@ -110,90 +114,89 @@ def tile_picked_yrwmd_sim_p_kernel(tc, x_words, x_scales, hT, qn, own, idf, bag,
         hb = {}
 
         def round_h(o, c):
-            name = "h%d%d" % (o, c)
-            hb[(o, c)] = round_and_group(name, raw[(o, c)], TC, name + "_b")
+            name = "h%d%d_b" % (o, c)
+            if (o, c) == (1, 0):
+                grouped = reuse2.tile([P, PACK * TC], BF16, name=name, offset=1024, align_bytes=64)
+            else:
+                grouped = keep.tile([P, PACK * TC], BF16, name=name, align_bytes=64)
+            hb[(o, c)] = round_and_group(grouped, raw[(o, c)])
 
         def quantize_h(o, c, tag):
             hq[(o, c)] = quantize("h%d%d" % (o, c), hb[(o, c)], TC, tag)
 
         raw = {(0, 0): h00[:]}
-        gather_words(0, 0, xw0, "xg00")
-        qg = keep.tile([P, S], F32, name="qg", tag="qg", align_bytes=64)
+        xg0 = gather_words(0, xw0)
+        qg = keep.tile([P, S], F32, name="qg", align_bytes=64)
         nc.vector.tensor_copy(qg[:], qw[:].indirect(offsets[:]))
-        gather_words(0, 1, xw0, "wq")
+        deal_words(0, xg0, 0, reuse.tile([P, 4, G], U32, name="xd00", offset=0, align_bytes=64))
+        deal_words(0, xg0, 1, keep.tile([P, 4, G], U32, name="xd01", tag="xd01", align_bytes=64))
         round_h(0, 0)
-        quantize_h(0, 0, "h00_c")
+        quantize_h(0, 0, "xg0")
 
-        late = keep.tile([P, T + S], F32, name="late", tag="h00", align_bytes=64)
-        for n, (o, c) in enumerate([(1, 0), (0, 1), (1, 1)]):
+        late = keep.tile([P, 2048], F32, name="late", tag="h00", align_bytes=64)
+        for n, (o, c) in enumerate([(1, 0), (0, 1)]):
             raw[(o, c)] = late[:, 1024 * n:1024 * (n + 1)]
             nc.sync.dma_start(raw[(o, c)].rearrange("p (j t) -> p j t", j=PACK), h_rows(o, c))
-        bag_raw = late[:, 3072:3584]
+        last = reuse.tile([P, 2048], F32, name="last", offset=2048, align_bytes=64)
+        raw[(1, 1)] = last[:, 0:1024]
+        nc.sync.dma_start(raw[(1, 1)].rearrange("p (j t) -> p j t", j=PACK), h_rows(1, 1))
+        bag_raw = last[:, 1024:1536]
         nc.sync.dma_start(bag_raw, bag.rearrange("(p j) m -> p (j m)", j=PACK))
-        own_t = late[:, 3584:3588]
-        idf_t = late[:, 3600:3604]
+        own_t = last[:, 1536:1540]
+        idf_t = last[:, 1552:1556]
         nc.sync.dma_start(own_t, own.rearrange("(p i) o -> p (i o)", i=PACK))
         nc.sync.dma_start(idf_t, idf.rearrange("(p i) o -> p (i o)", i=PACK))
 
-        qp = late[:, T:T + S]
-        for h in range(HALVES):
-            nc.scalar.activation(
-                qp[:, 512 * h:512 * (h + 1)].rearrange("p (f g e) -> p f g e", f=PAIRS, e=2),
-                qg[:, 512 * h:512 * (h + 1)].rearrange("p (g f e) -> p f g e", f=PAIRS, e=2),
-                ACT.Copy, scale=-1.0 / 1.5)
-        sp.append(keep.tile([P, S], U8, name="sp1", tag="qg", align_bytes=64))
-        nc.vector.memset(sp[1][:].bitcast(I32), 0)
-        place_scales(1)
-        nq = keep.tile([P, HALVES * PAIRS], F32, name="nq")
-        for h in range(HALVES):
-            qt = psum.tile([P, PAIRS, P], F32, name="qt", tag="bank")
-            for f in range(PAIRS):
-                nc.tensor.transpose(qt[:, f, :], qp[:, 512 * h + P * f:512 * h + P * (f + 1)], ident[:])
-            nc.scalar.copy(nq[:, PAIRS * h:PAIRS * (h + 1)], qt[:, :, 0])
+        nq = keep.tile([P, D], F32, name="nq")
+        by_word = qg[:].rearrange("p (g d) -> p d g", d=D)
+        for b in range(2):
+            qt = psum.tile([P, 4, P], F32, name="qt", tag="bank")
+            for f in range(4):
+                nc.tensor.transpose(qt[:, f, :], by_word[:, 4 * b + f, :], ident[:])
+            nc.scalar.activation(nq[:, 4 * b:4 * (b + 1)], qt[:, :, 0], ACT.Copy, scale=-1.0 / 1.5)
 
         banks = {}
 
-        def product(o, c):
+        def product(o, c, d):
             codes, scales = hq[(o, c)]
-            for f in range(PAIRS):
-                for h in range(HALVES):
-                    if o == 0:
-                        banks[(c, h, f)] = psum.tile([P, TC], F32, name="s", tag="bank")
-                    col = 512 * h + P * f
-                    nc.tensor.matmul_mx(
-                        out=banks[(c, h, f)][:],
-                        lhsT=xg[(o, h)][:, P * f:P * (f + 1)].bitcast(FP8X4),
-                        lhsT_scale=sp[o][:, col:col + P],
-                        rhs=codes[:].bitcast(FP8X4), rhs_scale=scales[:],
-                        start=(o == 0), stop=(o == PASSES - 1))
+            if o == 0:
+                banks[(c, d)] = psum.tile([P, TC], F32, name="s", tag="bank")
+            nc.tensor.matmul_mx(
+                out=banks[(c, d)][:],
+                lhsT=xd[(o, d // 4)][:, d % 4, :].bitcast(FP8X4),
+                lhsT_scale=sp[o][:, G * d:G * (d + 1)],
+                rhs=codes[:].bitcast(FP8X4), rhs_scale=scales[:],
+                start=(o == 0), stop=(o == PASSES - 1))
 
-        best = [keep.tile([P, PACK, P], F32, name="best%d" % h) for h in range(HALVES)]
-
+        best = keep.tile([P, PACK, P], F32, name="best")
         run = {}
 
         def nearest(c, f):
-            for h in range(HALVES):
-                sums = banks[(c, h, f)][:].rearrange("p (m i) -> p i m", i=PACK)
-                bias = nq[:, PAIRS * h + f:PAIRS * h + f + 1]
-                if f == PAIRS - 1:
-                    dst = best[h][:, :, 64 * c:64 * (c + 1)]
-                else:
-                    part = keep.tile([P, PACK, 64], F32, name="part%d%d%d" % (c, h, f), align_bytes=64)
-                    dst = part[:]
+            for b in range(2):
+                d = 2 * f + b
+                sums = banks[(c, d)][:].rearrange("p (m i) -> p i m", i=PACK)
+                bias = nq[:, d:d + 1]
+                part = keep.tile([P, PACK, 64], F32, name="part%d%d%d" % (c, b, f), align_bytes=64)
                 if f > 0:
-                    nc.vector.scalar_tensor_tensor(dst, sums, bias, run[h], ALU.add, ALU.max)
+                    nc.vector.scalar_tensor_tensor(part[:], sums, bias, run[b], ALU.add, ALU.max)
                 elif c == 0:
-                    nc.vector.tensor_scalar(dst, sums, bias, None, ALU.add)
+                    nc.vector.tensor_scalar(part[:], sums, bias, None, ALU.add)
                 else:
-                    nc.scalar.activation(dst, sums, ACT.Identity, bias=bias)
-                run[h] = dst
+                    nc.scalar.activation(part[:], sums, ACT.Identity, bias=bias)
+                run[b] = part[:]
 
-        product(0, 0)
-        for h in range(HALVES):
-            gather_words(1, h, xw1, "xg1%d" % h)
+        def join(c):
+            nc.vector.tensor_tensor(best[:, :, 64 * c:64 * (c + 1)], run[0], run[1], ALU.max)
+
+        for d in range(D):
+            product(0, 0, d)
+        xg1 = gather_words(1, xw1)
         round_h(1, 0)
         quantize_h(1, 0, "h10_c")
-        product(1, 0)
+        deal_words(1, xg1, 0, reuse2.tile([P, 4, G], U32, name="xd10", offset=0, align_bytes=64))
+        deal_words(1, xg1, 1, reuse2.tile([P, 4, G], U32, name="xd11", offset=2048, align_bytes=64))
+        for d in range(D):
+            product(1, 0, d)
         round_h(0, 1)
         round_h(1, 1)
         nearest(0, 0)
@@ -202,30 +205,27 @@ def tile_picked_yrwmd_sim_p_kernel(tc, x_words, x_scales, hT, qn, own, idf, bag,
         nearest(0, 2)
         quantize_h(1, 1, "part001")
         nearest(0, 3)
-        product(0, 1)
-        product(1, 1)
-        for f in range(PAIRS):
+        join(0)
+        for d in range(D):
+            for o in range(PASSES):
+                product(o, 1, d)
+        for f in range(4):
             nearest(1, f)
-        bag_c, bag_s = quantize("bag", round_and_group("bag", bag_raw, N, "part110"), N, "bag_c")
+        bag_c, bag_s = quantize("bag", round_and_group(keep.tile([P, PACK * N], BF16, name="bag_b", tag="part110", align_bytes=64), bag_raw), N, "part102")
+        join(1)
 
         z = keep.tile([P, N * PACK], BF16, name="z", align_bytes=64)
-        roots = []
+        dist = keep.tile([P, PACK, G], F32, name="dist")
+        for i in range(PACK):
+            turned = psum.tile([P, G], F32, name="turned", tag="bank")
+            nc.tensor.transpose(turned[:], best[:, i, :], ident[:])
+            nc.scalar.activation(dist[:, i, :], turned[:], ACT.Relu, bias=own_t[:, i:i + 1], scale=-1.5)
         for h in range(HALVES):
-            turned = psum.tile([P, PACK, P], F32, name="turned", tag="bank")
-            for i in range(PACK):
-                nc.tensor.transpose(turned[:, i, :], best[h][:, i, :], ident[:])
-            near = keep.tile([P, PACK, GH], F32, name="near%d" % h)
-            nc.vector.tensor_reduce(near[:], turned[:].rearrange("p i (g e) -> p i g e", e=2), AX.X, ALU.max)
-            dist = keep.tile([P, PACK, GH], F32, name="dist%d" % h)
-            for i in range(PACK):
-                nc.scalar.activation(dist[:, i, :], near[:, i, :], ACT.Relu, bias=own_t[:, i:i + 1], scale=-1.5)
             root = keep.tile([P, PACK, GH], F32, name="root%d" % h)
-            nc.scalar.activation(root[:], dist[:], ACT.Sqrt, bias=0.01)
-            roots.append(root)
-        for h in range(HALVES):
+            nc.scalar.activation(root[:], dist[:, :, GH * h:GH * (h + 1)], ACT.Sqrt, bias=0.01)
             nc.vector.tensor_tensor(
                 z[:, PACK * GH * h:PACK * GH * (h + 1)].rearrange("p (g i) -> p g i", i=PACK),
-                roots[h][:].rearrange("p i g -> p g i"),
+                root[:].rearrange("p i g -> p g i"),
                 idf_t.unsqueeze(1).to_broadcast([P, GH, PACK]), ALU.mult)
         z_c, z_s = quantize("z", z, N, "z_c")
         cost = psum.tile([P, N], F32, name="cost", tag="bank")

@@ -23,7 +23,6 @@ PACK = 4
 PASSES = 2
 HALVES = 2
 GH = 64
-G = 128
 PAIRS = 4
 TC = 256
 CHUNKS = 2
@@ -35,7 +34,6 @@ def tile_picked_yrwmd_sim_p_kernel(tc, x_words, x_scales, hT, qn, own, idf, bag,
         held = ctx.enter_context(tc.tile_pool(name="held", bufs=1))
         keep = ctx.enter_context(tc.tile_pool(name="keep", bufs=1))
         reuse = ctx.enter_context(tc.tile_pool(name="reuse", bufs=1))
-        reuse2 = ctx.enter_context(tc.tile_pool(name="reuse2", bufs=1))
         psum = ctx.enter_context(tc.psum_pool(name="psum", bufs=8))
 
         offsets = held.tile([P, S // 16], U16, name="offsets")
@@ -58,8 +56,8 @@ def tile_picked_yrwmd_sim_p_kernel(tc, x_words, x_scales, hT, qn, own, idf, bag,
         qw = reuse.tile([P, T], F32, name="qw", offset=0, align_bytes=64)
         zero = keep.tile([P, 1], F32, name="zero", tag="w1", align_bytes=64)
         nc.vector.memset(zero[:], 0.0)
-        warm = keep.tile([P, 1], F32, name="warm")
-        nc.scalar.activation(warm[:], zero[:], ACT.Sqrt, bias=1.0)
+        floor = keep.tile([P, 1], F32, name="floor")
+        nc.scalar.activation(floor[:], zero[:], ACT.Sqrt, bias=1e-4)
         nc.scalar.copy(qw[:, 0:2048], zero[:].to_broadcast([P, 2048]))
         nc.vector.memset(sw[32:64, :].bitcast(I32), 0)
         nc.vector.memset(sw[64:128, :].bitcast(I32), 0)
@@ -76,7 +74,9 @@ def tile_picked_yrwmd_sim_p_kernel(tc, x_words, x_scales, hT, qn, own, idf, bag,
         sg = keep.tile([P, S], U8, name="sg", align_bytes=64)
         nc.vector.tensor_copy(sg[:], sw[:].indirect(offsets[:]))
         sd = keep.tile([P, S], U8, name="sd", align_bytes=64)
-        nc.vector.tensor_copy(sd[:].rearrange("p (d g) -> p d g", d=D), sg[:].rearrange("p (g d) -> p d g", d=D))
+        nc.vector.tensor_copy(
+            sd[:].rearrange("p (h f g e) -> p h f g e", h=HALVES, f=PAIRS, e=2),
+            sg[:].rearrange("p (h g f e) -> p h f g e", h=HALVES, f=PAIRS, e=2))
         sp = [sd, sp1]
         moves = [(o, q) for o in range(PASSES) for q in range(4) if (o, q) != (0, 0)]
         for n, (o, q) in enumerate(moves):
@@ -84,27 +84,25 @@ def tile_picked_yrwmd_sim_p_kernel(tc, x_words, x_scales, hT, qn, own, idf, bag,
             queue.dma_start(sp[o][32 * q:32 * q + 4, :].bitcast(I32),
                             sd[16 * o + 4 * q:16 * o + 4 * q + 4, :].bitcast(I32))
 
-        xd = {}
+        xg = {}
 
-        def gather_words(o, w):
-            t = keep.tile([P, S], U32, name="xg%d" % o, align_bytes=64)
-            nc.vector.tensor_copy(t[:], w[:].indirect(offsets[:]))
-            return t
-
-        def deal_words(o, picked, u, t):
+        def gather_words(o, h, w, t):
             nc.vector.tensor_copy(
-                t[:].bitcast(I32).rearrange("p d (b g) -> p b d g", g=4),
-                picked[:].bitcast(I32).rearrange("p (b g d) -> p b d g", g=4, d=D)[:, :, 4 * u:4 * (u + 1), :])
-            xd[(o, u)] = t
+                t[:].rearrange("p (f g e) -> p g f e", f=PAIRS, e=2),
+                w[:].indirect(offsets[:, 32 * h:32 * (h + 1)]))
+            xg[(o, h)] = t
 
-        def round_and_group(grouped, src):
+        def round_and_group(name, src, width, tag):
+            grouped = keep.tile([P, PACK * width], BF16, name=name + "_b", tag=tag, align_bytes=64)
             nc.scalar.copy(
                 grouped[:].rearrange("p (c i j) -> p c j i", i=4, j=PACK),
                 src.rearrange("p (j c i) -> p c j i", i=4, j=PACK))
             return grouped
 
-        def quantize(name, grouped, width, tag):
-            codes = keep.tile([P, width], U32, name=name + "_c", tag=tag, align_bytes=64)
+        def codes_tile(name, width, tag):
+            return keep.tile([P, width], U32, name=name + "_c", tag=tag, align_bytes=64)
+
+        def quantize(name, grouped, width, codes):
             scales = keep.tile([P, width], U8, name=name + "_s", align_bytes=64)
             nc.vector.quantize_mx(out=codes[:].bitcast(FP8X4), scales=scales[:], in_=grouped[:])
             return codes, scales
@@ -114,30 +112,25 @@ def tile_picked_yrwmd_sim_p_kernel(tc, x_words, x_scales, hT, qn, own, idf, bag,
         hb = {}
 
         def round_h(o, c):
-            name = "h%d%d_b" % (o, c)
-            if (o, c) == (1, 0):
-                grouped = reuse2.tile([P, PACK * TC], BF16, name=name, offset=1024, align_bytes=64)
-            else:
-                grouped = keep.tile([P, PACK * TC], BF16, name=name, align_bytes=64)
-            hb[(o, c)] = round_and_group(grouped, raw[(o, c)])
+            name = "h%d%d" % (o, c)
+            hb[(o, c)] = round_and_group(name, raw[(o, c)], TC, name + "_b")
 
-        def quantize_h(o, c, tag):
-            hq[(o, c)] = quantize("h%d%d" % (o, c), hb[(o, c)], TC, tag)
+        def quantize_h(o, c, codes):
+            hq[(o, c)] = quantize("h%d%d" % (o, c), hb[(o, c)], TC, codes)
 
         raw = {(0, 0): h00[:]}
-        xg0 = gather_words(0, xw0)
+        gather_words(0, 0, xw0, keep.tile([P, 512], U32, name="xg00", align_bytes=64))
         qg = keep.tile([P, S], F32, name="qg", align_bytes=64)
         nc.vector.tensor_copy(qg[:], qw[:].indirect(offsets[:]))
-        deal_words(0, xg0, 0, reuse.tile([P, 4, G], U32, name="xd00", offset=0, align_bytes=64))
-        deal_words(0, xg0, 1, keep.tile([P, 4, G], U32, name="xd01", tag="xd01", align_bytes=64))
+        gather_words(0, 1, xw0, reuse.tile([P, 512], U32, name="xg01", offset=0, align_bytes=64))
         round_h(0, 0)
-        quantize_h(0, 0, "xg0")
+        quantize_h(0, 0, reuse.tile([P, TC], U32, name="h00_c", offset=2048, align_bytes=64))
 
-        late = keep.tile([P, 2048], F32, name="late", tag="h00", align_bytes=64)
+        late = keep.tile([P, 3072], F32, name="late", tag="h00", align_bytes=64)
         for n, (o, c) in enumerate([(1, 0), (0, 1)]):
             raw[(o, c)] = late[:, 1024 * n:1024 * (n + 1)]
             nc.sync.dma_start(raw[(o, c)].rearrange("p (j t) -> p j t", j=PACK), h_rows(o, c))
-        last = reuse.tile([P, 2048], F32, name="last", offset=2048, align_bytes=64)
+        last = reuse.tile([P, 2048], F32, name="last", offset=4096, align_bytes=64)
         raw[(1, 1)] = last[:, 0:1024]
         nc.sync.dma_start(raw[(1, 1)].rearrange("p (j t) -> p j t", j=PACK), h_rows(1, 1))
         bag_raw = last[:, 1024:1536]
@@ -147,87 +140,98 @@ def tile_picked_yrwmd_sim_p_kernel(tc, x_words, x_scales, hT, qn, own, idf, bag,
         nc.sync.dma_start(own_t, own.rearrange("(p i) o -> p (i o)", i=PACK))
         nc.sync.dma_start(idf_t, idf.rearrange("(p i) o -> p (i o)", i=PACK))
 
-        nq = keep.tile([P, D], F32, name="nq")
-        by_word = qg[:].rearrange("p (g d) -> p d g", d=D)
-        for b in range(2):
-            qt = psum.tile([P, 4, P], F32, name="qt", tag="bank")
-            for f in range(4):
-                nc.tensor.transpose(qt[:, f, :], by_word[:, 4 * b + f, :], ident[:])
-            nc.scalar.activation(nq[:, 4 * b:4 * (b + 1)], qt[:, :, 0], ACT.Copy, scale=-1.0 / 1.5)
+        qp = late[:, 2048:3072]
+        for h in range(HALVES):
+            nc.scalar.activation(
+                qp[:, 512 * h:512 * (h + 1)].rearrange("p (f g e) -> p f g e", f=PAIRS, e=2),
+                qg[:, 512 * h:512 * (h + 1)].rearrange("p (g f e) -> p f g e", f=PAIRS, e=2),
+                ACT.Copy, scale=-1.0 / 1.5)
+        nq = keep.tile([P, HALVES * PAIRS], F32, name="nq")
+        for h in range(HALVES):
+            qt = psum.tile([P, PAIRS, P], F32, name="qt", tag="bank")
+            for f in range(PAIRS):
+                nc.tensor.transpose(qt[:, f, :], qp[:, 512 * h + P * f:512 * h + P * (f + 1)], ident[:])
+            nc.scalar.copy(nq[:, PAIRS * h:PAIRS * (h + 1)], qt[:, :, 0])
 
         banks = {}
 
-        def product(o, c, d):
+        def product(o, c, f, h):
             codes, scales = hq[(o, c)]
             if o == 0:
-                banks[(c, d)] = psum.tile([P, TC], F32, name="s", tag="bank")
+                banks[(c, h, f)] = psum.tile([P, TC], F32, name="s", tag="bank")
+            col = 512 * h + P * f
             nc.tensor.matmul_mx(
-                out=banks[(c, d)][:],
-                lhsT=xd[(o, d // 4)][:, d % 4, :].bitcast(FP8X4),
-                lhsT_scale=sp[o][:, G * d:G * (d + 1)],
+                out=banks[(c, h, f)][:],
+                lhsT=xg[(o, h)][:, P * f:P * (f + 1)].bitcast(FP8X4),
+                lhsT_scale=sp[o][:, col:col + P],
                 rhs=codes[:].bitcast(FP8X4), rhs_scale=scales[:],
                 start=(o == 0), stop=(o == PASSES - 1))
 
-        best = keep.tile([P, PACK, P], F32, name="best")
+        tiles = [(f, h) for f in range(PAIRS) for h in range(HALVES)]
+        best = [keep.tile([P, PACK, P], F32, name="best%d" % h) for h in range(HALVES)]
+
         run = {}
 
         def nearest(c, f):
-            for b in range(2):
-                d = 2 * f + b
-                sums = banks[(c, d)][:].rearrange("p (m i) -> p i m", i=PACK)
-                bias = nq[:, d:d + 1]
-                part = keep.tile([P, PACK, 64], F32, name="part%d%d%d" % (c, b, f), align_bytes=64)
-                if f > 0:
-                    nc.vector.scalar_tensor_tensor(part[:], sums, bias, run[b], ALU.add, ALU.max)
-                elif c == 0:
-                    nc.vector.tensor_scalar(part[:], sums, bias, None, ALU.add)
+            for h in range(HALVES):
+                sums = banks[(c, h, f)][:].rearrange("p (m i) -> p i m", i=PACK)
+                bias = nq[:, PAIRS * h + f:PAIRS * h + f + 1]
+                if f == PAIRS - 1:
+                    dst = best[h][:, :, 64 * c:64 * (c + 1)]
                 else:
-                    nc.scalar.activation(part[:], sums, ACT.Identity, bias=bias)
-                run[b] = part[:]
+                    part = keep.tile([P, PACK, 64], F32, name="part%d%d%d" % (c, h, f), align_bytes=64)
+                    dst = part[:]
+                if f > 0:
+                    nc.vector.scalar_tensor_tensor(dst, sums, bias, run[h], ALU.add, ALU.max)
+                elif c == 0:
+                    nc.vector.tensor_scalar(dst, sums, bias, None, ALU.add)
+                else:
+                    nc.scalar.activation(dst, sums, ACT.Identity, bias=bias)
+                run[h] = dst
 
-        def join(c):
-            nc.vector.tensor_tensor(best[:, :, 64 * c:64 * (c + 1)], run[0], run[1], ALU.max)
-
-        for d in range(D):
-            product(0, 0, d)
-        xg1 = gather_words(1, xw1)
+        for f, h in tiles:
+            product(0, 0, f, h)
+        for h in range(HALVES):
+            gather_words(1, h, xw1, keep.tile([P, 512], U32, name="xg1%d" % h, align_bytes=64))
         round_h(1, 0)
-        quantize_h(1, 0, "h10_c")
-        deal_words(1, xg1, 0, reuse2.tile([P, 4, G], U32, name="xd10", offset=0, align_bytes=64))
-        deal_words(1, xg1, 1, reuse2.tile([P, 4, G], U32, name="xd11", offset=2048, align_bytes=64))
-        for d in range(D):
-            product(1, 0, d)
+        quantize_h(1, 0, codes_tile("h10", TC, "h10_c"))
+        for f, h in tiles:
+            product(1, 0, f, h)
         round_h(0, 1)
         round_h(1, 1)
         nearest(0, 0)
         nearest(0, 1)
-        quantize_h(0, 1, "part000")
+        quantize_h(0, 1, codes_tile("h01", TC, "part000"))
         nearest(0, 2)
-        quantize_h(1, 1, "part001")
+        quantize_h(1, 1, codes_tile("h11", TC, "part001"))
         nearest(0, 3)
-        join(0)
-        for d in range(D):
+        for f, h in tiles:
             for o in range(PASSES):
-                product(o, 1, d)
-        for f in range(4):
+                product(o, 1, f, h)
+        for f in range(PAIRS):
             nearest(1, f)
-        bag_c, bag_s = quantize("bag", round_and_group(keep.tile([P, PACK * N], BF16, name="bag_b", tag="part110", align_bytes=64), bag_raw), N, "part102")
-        join(1)
+        bag_c, bag_s = quantize("bag", round_and_group("bag", bag_raw, N, "part110"), N, codes_tile("bag", N, "bag_c"))
 
         z = keep.tile([P, N * PACK], BF16, name="z", align_bytes=64)
-        dist = keep.tile([P, PACK, G], F32, name="dist")
-        for i in range(PACK):
-            turned = psum.tile([P, G], F32, name="turned", tag="bank")
-            nc.tensor.transpose(turned[:], best[:, i, :], ident[:])
-            nc.scalar.activation(dist[:, i, :], turned[:], ACT.Relu, bias=own_t[:, i:i + 1], scale=-1.5)
+        roots = []
         for h in range(HALVES):
+            turned = psum.tile([P, PACK, P], F32, name="turned", tag="bank")
+            for i in range(PACK):
+                nc.tensor.transpose(turned[:, i, :], best[h][:, i, :], ident[:])
+            near = keep.tile([P, PACK, GH], F32, name="near%d" % h)
+            nc.vector.tensor_reduce(near[:], turned[:].rearrange("p i (g e) -> p i g e", e=2), AX.X, ALU.max)
+            dist = keep.tile([P, PACK, GH], F32, name="dist%d" % h)
+            for i in range(PACK):
+                nc.scalar.activation(dist[:, i, :], near[:, i, :], ACT.Relu, bias=own_t[:, i:i + 1], scale=-1.5)
             root = keep.tile([P, PACK, GH], F32, name="root%d" % h)
-            nc.scalar.activation(root[:], dist[:, :, GH * h:GH * (h + 1)], ACT.Sqrt, bias=0.01)
+            nc.scalar.activation(root[:], dist[:], ACT.Sqrt, bias=floor[:])
+            roots.append(root)
+        for h in range(HALVES):
             nc.vector.tensor_tensor(
                 z[:, PACK * GH * h:PACK * GH * (h + 1)].rearrange("p (g i) -> p g i", i=PACK),
-                root[:].rearrange("p i g -> p g i"),
+                roots[h][:].rearrange("p i g -> p g i"),
                 idf_t.unsqueeze(1).to_broadcast([P, GH, PACK]), ALU.mult)
-        z_c, z_s = quantize("z", z, N, "z_c")
+        z_c, z_s = quantize("z", z, N, codes_tile("z", N, "z_c"))
         cost = psum.tile([P, N], F32, name="cost", tag="bank")
         nc.tensor.matmul_mx(out=cost[:], lhsT=bag_c[:].bitcast(FP8X4), lhsT_scale=bag_s[:],
                             rhs=z_c[:].bitcast(FP8X4), rhs_scale=z_s[:], start=True, stop=True)

from contextlib import ExitStack

import concourse.mybir as mybir
from concourse.masks import make_identity

K, T, S, V, D, N = 1024, 4096, 1024, 512, 8, 128
FLOPS = 2 * K * V * S + 2 * V * N * (S // D)
BYTES = K * T + (K // 32) * T + 4 * (K * V + T + 2 * V + V * N + N * (S // D)) + 2 * 128 * (S // 16)

F32 = mybir.dt.float32
BF16 = mybir.dt.bfloat16
I32 = mybir.dt.int32
U32 = mybir.dt.uint32
U16 = mybir.dt.uint16
U8 = mybir.dt.uint8
FP8X4 = mybir.dt.float8_e4m3fn_x4
ALU = mybir.AluOpType
ACT = mybir.ActivationFunctionType
AX = mybir.AxisListType

P = 128
PACK = 4
PASSES = 2
HALVES = 2
GH = 64
PAIRS = 4
TC = 256
CHUNKS = 2


def tile_picked_yrwmd_sim_p_kernel(tc, x_words, x_scales, hT, qn, own, idf, bag, offs, out):
    nc = tc.nc
    with ExitStack() as ctx:
        held = ctx.enter_context(tc.tile_pool(name="held", bufs=1))
        keep = ctx.enter_context(tc.tile_pool(name="keep", bufs=1))
        reuse = ctx.enter_context(tc.tile_pool(name="reuse", bufs=1))
        psum = ctx.enter_context(tc.psum_pool(name="psum", bufs=8))

        offsets = held.tile([P, S // 16], U16, name="offsets")
        nc.sync.dma_start(offsets[:], offs)

        def load_words(o, tag):
            w = keep.tile([P, T], U32, name="xw%d" % o, tag=tag, align_bytes=64)
            nc.sync.dma_start(w[:].bitcast(I32), x_words[o].rearrange("p c r -> p (c r)").bitcast(I32))
            return w

        def h_rows(o, c):
            return hT[512 * o:512 * (o + 1), TC * c:TC * (c + 1)].rearrange("(p j) t -> p j t", j=PACK)

        sw = keep.tile([P, T], U8, name="sw", align_bytes=64)
        nc.sync.dma_start(sw[0:32, :].bitcast(I32), x_scales.rearrange("o q c -> (o q) c").bitcast(I32))
        xw0 = load_words(0, "w0")
        h00 = keep.tile([P, PACK * TC], F32, name="h00", tag="h00", align_bytes=64)
        nc.sync.dma_start(h00[:].rearrange("p (j t) -> p j t", j=PACK), h_rows(0, 0))

        qw = reuse.tile([P, T], F32, name="qw", offset=0, align_bytes=64)
        zero = keep.tile([P, 1], F32, name="zero", tag="w1", align_bytes=64)
        nc.vector.memset(zero[:], 0.0)
        floor = keep.tile([P, 1], F32, name="floor")
        nc.scalar.activation(floor[:], zero[:], ACT.Sqrt, bias=1e-4)
        nc.scalar.copy(qw[:, 0:2048], zero[:].to_broadcast([P, 2048]))
        nc.vector.memset(sw[32:64, :].bitcast(I32), 0)
        nc.vector.memset(sw[64:128, :].bitcast(I32), 0)
        nc.vector.memset(qw[:, 2048:3072], 0.0)
        nc.gpsimd.memset(qw[:, 3072:4096], 0.0)
        nc.sync.dma_start(qw[0:1, :], qn[0:1, :])
        xw1 = load_words(1, "w1")

        sp1 = keep.tile([P, S], U8, name="sp1", align_bytes=64)
        nc.gpsimd.memset(sp1[:].bitcast(I32), 0)
        ident = keep.tile([P, P], F32, name="ident")
        make_identity(nc, ident[:])

        sg = keep.tile([P, S], U8, name="sg", align_bytes=64)
        nc.vector.tensor_copy(sg[:], sw[:].indirect(offsets[:]))
        sd = keep.tile([P, S], U8, name="sd", align_bytes=64)
        nc.vector.tensor_copy(
            sd[:].rearrange("p (h f g e) -> p h f g e", h=HALVES, f=PAIRS, e=2),
            sg[:].rearrange("p (h g f e) -> p h f g e", h=HALVES, f=PAIRS, e=2))
        sp = [sd, sp1]
        moves = [(o, q) for o in range(PASSES) for q in range(4) if (o, q) != (0, 0)]
        for n, (o, q) in enumerate(moves):
            queue = nc.scalar if n < 4 else nc.gpsimd
            queue.dma_start(sp[o][32 * q:32 * q + 4, :].bitcast(I32),
                            sd[16 * o + 4 * q:16 * o + 4 * q + 4, :].bitcast(I32))

        xg = {}

        def gather_words(o, h, w, t):
            nc.vector.tensor_copy(
                t[:].rearrange("p (f g e) -> p g f e", f=PAIRS, e=2),
                w[:].indirect(offsets[:, 32 * h:32 * (h + 1)]))
            xg[(o, h)] = t

        def round_and_group(name, src, width, tag):
            grouped = keep.tile([P, PACK * width], BF16, name=name + "_b", tag=tag, align_bytes=64)
            nc.scalar.copy(
                grouped[:].rearrange("p (c i j) -> p c j i", i=4, j=PACK),
                src.rearrange("p (j c i) -> p c j i", i=4, j=PACK))
            return grouped

        def codes_tile(name, width, tag):
            return keep.tile([P, width], U32, name=name + "_c", tag=tag, align_bytes=64)

        def quantize(name, grouped, width, codes):
            scales = keep.tile([P, width], U8, name=name + "_s", align_bytes=64)
            nc.vector.quantize_mx(out=codes[:].bitcast(FP8X4), scales=scales[:], in_=grouped[:])
            return codes, scales

        hq = {}

        hb = {}

        def round_h(o, c):
            name = "h%d%d" % (o, c)
            hb[(o, c)] = round_and_group(name, raw[(o, c)], TC, name + "_b")

        def quantize_h(o, c, codes):
            hq[(o, c)] = quantize("h%d%d" % (o, c), hb[(o, c)], TC, codes)

        raw = {(0, 0): h00[:]}
        gather_words(0, 0, xw0, keep.tile([P, 512], U32, name="xg00", align_bytes=64))
        qg = keep.tile([P, S], F32, name="qg", align_bytes=64)
        nc.vector.tensor_copy(qg[:], qw[:].indirect(offsets[:]))
        gather_words(0, 1, xw0, reuse.tile([P, 512], U32, name="xg01", offset=0, align_bytes=64))
        round_h(0, 0)
        quantize_h(0, 0, reuse.tile([P, TC], U32, name="h00_c", offset=2048, align_bytes=64))

        late = keep.tile([P, 3072], F32, name="late", tag="h00", align_bytes=64)
        for n, (o, c) in enumerate([(1, 0), (0, 1)]):
            raw[(o, c)] = late[:, 1024 * n:1024 * (n + 1)]
            nc.sync.dma_start(raw[(o, c)].rearrange("p (j t) -> p j t", j=PACK), h_rows(o, c))
        last = reuse.tile([P, 2048], F32, name="last", offset=4096, align_bytes=64)
        raw[(1, 1)] = last[:, 0:1024]
        nc.sync.dma_start(raw[(1, 1)].rearrange("p (j t) -> p j t", j=PACK), h_rows(1, 1))
        bag_raw = last[:, 1024:1536]
        nc.sync.dma_start(bag_raw, bag.rearrange("(p j) m -> p (j m)", j=PACK))
        own_t = last[:, 1536:1540]
        idf_t = last[:, 1552:1556]
        nc.sync.dma_start(own_t, own.rearrange("(p i) o -> p (i o)", i=PACK))
        nc.sync.dma_start(idf_t, idf.rearrange("(p i) o -> p (i o)", i=PACK))

        qp = late[:, 2048:3072]
        for h in range(HALVES):
            nc.scalar.activation(
                qp[:, 512 * h:512 * (h + 1)].rearrange("p (f g e) -> p f g e", f=PAIRS, e=2),
                qg[:, 512 * h:512 * (h + 1)].rearrange("p (g f e) -> p f g e", f=PAIRS, e=2),
                ACT.Copy, scale=-1.0 / 1.5)
        nq = keep.tile([P, HALVES * PAIRS], F32, name="nq")
        for h in range(HALVES):
            qt = psum.tile([P, PAIRS, P], F32, name="qt", tag="bank")
            for f in range(PAIRS):
                nc.tensor.transpose(qt[:, f, :], qp[:, 512 * h + P * f:512 * h + P * (f + 1)], ident[:])
            nc.scalar.copy(nq[:, PAIRS * h:PAIRS * (h + 1)], qt[:, :, 0])

        banks = {}

        def product(o, c, f, h):
            codes, scales = hq[(o, c)]
            if o == 0:
                banks[(c, h, f)] = psum.tile([P, TC], F32, name="s", tag="bank")
            col = 512 * h + P * f
            nc.tensor.matmul_mx(
                out=banks[(c, h, f)][:],
                lhsT=xg[(o, h)][:, P * f:P * (f + 1)].bitcast(FP8X4),
                lhsT_scale=sp[o][:, col:col + P],
                rhs=codes[:].bitcast(FP8X4), rhs_scale=scales[:],
                start=(o == 0), stop=(o == PASSES - 1))

        tiles = [(f, h) for f in range(PAIRS) for h in range(HALVES)]
        best = [keep.tile([P, PACK, P], F32, name="best%d" % h) for h in range(HALVES)]

        run = {}

        def nearest(c, f):
            for h in range(HALVES):
                sums = banks[(c, h, f)][:].rearrange("p (m i) -> p i m", i=PACK)
                bias = nq[:, PAIRS * h + f:PAIRS * h + f + 1]
                if f == PAIRS - 1:
                    dst = best[h][:, :, 64 * c:64 * (c + 1)]
                else:
                    part = keep.tile([P, PACK, 64], F32, name="part%d%d%d" % (c, h, f), align_bytes=64)
                    dst = part[:]
                if f > 0:
                    nc.vector.scalar_tensor_tensor(dst, sums, bias, run[h], ALU.add, ALU.max)
                elif c == 0:
                    nc.vector.tensor_scalar(dst, sums, bias, None, ALU.add)
                else:
                    nc.scalar.activation(dst, sums, ACT.Identity, bias=bias)
                run[h] = dst

        for f, h in tiles:
            product(0, 0, f, h)
        for h in range(HALVES):
            gather_words(1, h, xw1, keep.tile([P, 512], U32, name="xg1%d" % h, align_bytes=64))
        round_h(1, 0)
        quantize_h(1, 0, codes_tile("h10", TC, "h10_c"))
        for f, h in tiles:
            product(1, 0, f, h)
        round_h(0, 1)
        round_h(1, 1)
        nearest(0, 0)
        nearest(0, 1)
        quantize_h(0, 1, codes_tile("h01", TC, "part000"))
        nearest(0, 2)
        quantize_h(1, 1, codes_tile("h11", TC, "part001"))
        nearest(0, 3)
        for f, h in tiles:
            for o in range(PASSES):
                product(o, 1, f, h)
        for f in range(PAIRS):
            nearest(1, f)
        bag_c, bag_s = quantize("bag", round_and_group("bag", bag_raw, N, "part110"), N, codes_tile("bag", N, "bag_c"))

        z = keep.tile([P, N * PACK], BF16, name="z", align_bytes=64)
        roots = []
        for h in range(HALVES):
            turned = psum.tile([P, PACK, P], F32, name="turned", tag="bank")
            for i in range(PACK):
                nc.tensor.transpose(turned[:, i, :], best[h][:, i, :], ident[:])
            near = keep.tile([P, PACK, GH], F32, name="near%d" % h)
            nc.vector.tensor_reduce(near[:], turned[:].rearrange("p i (g e) -> p i g e", e=2), AX.X, ALU.max)
            dist = keep.tile([P, PACK, GH], F32, name="dist%d" % h)
            for i in range(PACK):
                nc.scalar.activation(dist[:, i, :], near[:, i, :], ACT.Relu, bias=own_t[:, i:i + 1], scale=-1.5)
            root = keep.tile([P, PACK, GH], F32, name="root%d" % h)
            nc.scalar.activation(root[:], dist[:], ACT.Sqrt, bias=floor[:])
            roots.append(root)
        for h in range(HALVES):
            nc.vector.tensor_tensor(
                z[:, PACK * GH * h:PACK * GH * (h + 1)].rearrange("p (g i) -> p g i", i=PACK),
                roots[h][:].rearrange("p i g -> p g i"),
                idf_t.unsqueeze(1).to_broadcast([P, GH, PACK]), ALU.mult)
        z_c, z_s = quantize("z", z, N, codes_tile("z", N, "z_c"))
        cost = psum.tile([P, N], F32, name="cost", tag="bank")
        nc.tensor.matmul_mx(out=cost[:], lhsT=bag_c[:].bitcast(FP8X4), lhsT_scale=bag_s[:],
                            rhs=z_c[:].bitcast(FP8X4), rhs_scale=z_s[:], start=True, stop=True)
        result = keep.tile([P, N], F32, name="result")
        nc.scalar.activation(result[:], cost[:], ACT.Exp, scale=-1.0)
        nc.sync.dma_start(out, result[:])
